import numpy as np
import ml_dtypes


def mxq(x, axis, fmt="e4m3"):
    dtype, down = {"e4m3": (ml_dtypes.float8_e4m3fn, 7), "e5m2": (ml_dtypes.float8_e5m2, 14)}[fmt]
    v = np.moveaxis(np.asarray(x, np.float32).astype(ml_dtypes.bfloat16).astype(np.float64), axis, -1)
    blocks = v.reshape(v.shape[:-1] + (-1, 32))
    amax = np.abs(blocks).max(-1, keepdims=True)
    byte = np.maximum(np.where(amax > 0, np.frexp(amax)[1] - 1 + 127, 0) - down, 1)
    scale = np.exp2(byte - 127.0)
    codes = (blocks / scale).astype(np.float32).astype(dtype).astype(np.float64)
    return np.moveaxis((codes * scale).reshape(v.shape), -1, axis)


WIDE = False


def mx_kscale(k):
    if not WIDE:
        return np.ones(k)
    levels = np.array([10, -10, 5, -5, 0])
    if k % 512:
        return np.exp2(np.random.permutation(np.resize(levels, k // 32))).repeat(32)
    a = np.empty((k // 512, 16))
    for p in range(k // 512):
        a[p, :8] = np.random.permutation(np.resize(levels, 8))
        for g in range(8):
            far = levels[np.abs(levels - a[p, g]) >= 10]
            a[p, g + 8] = far[np.random.randint(len(far))]
    return np.exp2(a.ravel()).repeat(32)


def f64(x):
    return np.asarray(x).astype(np.float64)


def striped8(idx):
    return np.asarray(idx).reshape(8, -1, 16).transpose(0, 2, 1).reshape(128, -1).astype(np.uint16)


def unstriped8(offs):
    return offs.reshape(8, 16, -1).transpose(0, 2, 1).reshape(8, -1).astype(np.int64)


def pick8(x, idx, run):
    r = np.arange(len(x))
    return x[r[:, None], idx[r % (8 * run) // run]]


E2M1 = np.array([0.0, 0.5, 1.0, 1.5, 2.0, 3.0, 4.0, 6.0, -0.0, -0.5, -1.0, -1.5, -2.0, -3.0, -4.0, -6.0])


def pack_weight(w, fmt):
    k, n = w.shape
    w = f64(np.asarray(w, np.float32).astype(ml_dtypes.bfloat16)).reshape(k // 32, 32, n)
    amax = np.abs(w).max(1)
    if fmt == "e4m3":
        byte = np.frexp(amax)[1] - 1 + 127 - 7
    else:
        mant, ex = np.frexp(amax / 6.0)
        byte = np.where(mant > 0.5, ex, ex - 1) + 127
    byte = np.clip(np.where(amax > 0, byte, 1), 1, 254)
    scaled = (w * np.exp2(127.0 - byte)[:, None, :]).reshape(k, n).astype(np.float32)
    by_word = np.ascontiguousarray(scaled.reshape(k // 512, 128, 4, n).transpose(0, 1, 3, 2))
    if fmt == "e4m3":
        words = by_word.astype(ml_dtypes.float8_e4m3fn).view(np.uint8)
    else:
        c = by_word.astype(ml_dtypes.float4_e2m1fn).view(np.uint8) & 0xF
        words = (c[..., 0::2] | (c[..., 1::2] << 4)).reshape(k // 512, 128, 2 * n)
    return np.ascontiguousarray(words), np.ascontiguousarray(byte.astype(np.uint8).reshape(k // 512, 16, n))


def unpack_weight(words, scales, fmt):
    g, _, n = scales.shape
    words = np.ascontiguousarray(words).reshape(g, 128, n, -1)
    if fmt == "e4m3":
        vals = words.view(ml_dtypes.float8_e4m3fn).astype(np.float64)
    else:
        nib = np.empty((g, 128, n, 4), np.uint8)
        nib[..., 0::2] = words & 0xF
        nib[..., 1::2] = words >> 4
        vals = E2M1[nib]
    vals = vals * np.repeat(np.exp2(scales.astype(np.float64) - 127.0), 8, axis=1)[..., None]
    return vals.transpose(0, 1, 3, 2).reshape(g * 512, n)


D, T, U, I, J, Q = 512, 1024, 1024, 512, 256, 128


def setup_inputs():
    n = np.random.standard_normal
    idx = np.stack([np.random.permutation(T)[:I] for _ in range(8)])
    idx2 = np.stack([np.random.permutation(U)[:J] for _ in range(8)])
    idx3 = np.stack([np.random.permutation(U)[:J] for _ in range(8)])
    idx4 = np.stack([np.random.permutation(U)[:I] for _ in range(8)])
    fd = mx_kscale(D)
    keysp = pack_weight(n((D, T)) / fd[:, None], "e4m3")
    notesp = pack_weight(n((D, U)) / fd[:, None], "e2m1")
    return {
        "query": (n((D, Q)) * 1.0 / np.sqrt(D) * fd[:, None]).astype(np.float32),
        "keys_words": keysp[0],
        "keys_scales": keysp[1],
        "notes_words": notesp[0],
        "notes_scales": notesp[1],
        "offs": striped8(idx),
        "offs2": striped8(idx2),
        "offs3": striped8(idx3),
        "offs4": striped8(idx4),
    }


def reference(query, keys_words, keys_scales, notes_words, notes_scales, offs, offs2, offs3, offs4):
    idx = unstriped8(offs)
    idx2 = unstriped8(offs2)
    idx3 = unstriped8(offs3)
    idx4 = unstriped8(offs4)
    keysu = unpack_weight(keys_words, keys_scales, "e4m3")
    notesu = unpack_weight(notes_words, notes_scales, "e2m1")
    queryq = mxq(f64(query), 0, "e4m3")
    a = queryq.T @ keysu
    b = queryq.T @ notesu
    w = pick8(a, idx, 16) * 0.75
    p2 = w.reshape(Q, J, I // J).sum(axis=2)
    v = p2 - pick8(b, idx2, 16)
    f1 = np.zeros((Q, U))
    f1[np.arange(Q)[:, None], idx3[np.arange(Q) % 128 // 16]] = v
    bb = b + f1
    y = pick8(bb, idx4, 16) + w
    return y

@@ -1,0 +1,135 @@
+from contextlib import ExitStack
+
+import concourse.mybir as mybir
+
+D, T, U, I, J, Q = 512, 1024, 1024, 512, 256, 128
+FLOPS = 2 * D * Q * (T + U)
+
+F32 = mybir.dt.float32
+BF16 = mybir.dt.bfloat16
+I32 = mybir.dt.int32
+U32 = mybir.dt.uint32
+U16 = mybir.dt.uint16
+U8 = mybir.dt.uint8
+FP8X4 = mybir.dt.float8_e4m3fn_x4
+FP4X4 = mybir.dt.float4_e2m1fn_x4
+ADD = mybir.AluOpType.add
+MULT = mybir.AluOpType.mult
+COPY = mybir.ActivationFunctionType.Copy
+
+P = 128
+PACK = 4
+PIECE = 256
+W_SCALE = 0.75
+
+
+def load_scale_rows(nc, plane, scales):
+    for quadrant in range(4):
+        nc.sync.dma_start(
+            out=plane[32 * quadrant : 32 * quadrant + 4, :].bitcast(I32),
+            in_=scales[0, 4 * quadrant : 4 * quadrant + 4, :].bitcast(I32),
+        )
+
+
+def tile_attend_pairspread_two_kernel(
+    tc, query, keys_words, keys_scales, notes_words, notes_scales, offs, offs2, offs3, offs4, out
+):
+    nc = tc.nc
+    with ExitStack() as ctx:
+        lists = ctx.enter_context(tc.tile_pool(name="lists", bufs=1))
+        sb = ctx.enter_context(tc.tile_pool(name="sb", bufs=1))
+        psum = ctx.enter_context(tc.psum_pool(name="psum", bufs=1))
+
+        token_list = lists.tile([P, I // 16], U16, name="token_list")
+        minus_list = lists.tile([P, J // 16], U16, name="minus_list")
+        spread_list = lists.tile([P, J // 16], U16, name="spread_list")
+        result_list = lists.tile([P, I // 16], U16, name="result_list")
+
+        q_raw = sb.tile([P, PACK, Q], F32, name="q_raw")
+        key_words = sb.tile([P, T], U32, name="key_words", align_bytes=64)
+        key_plane = sb.tile([P, T], U8, name="key_plane", align_bytes=64)
+        note_words = sb.tile([P, 2 * U], U8, name="note_words", align_bytes=64)
+        note_plane = sb.tile([P, U], U8, name="note_plane", align_bytes=64)
+        f1 = sb.tile([P, U], F32, name="f1")
+
+        nc.sync.dma_start(out=q_raw[:], in_=query.rearrange("(p j) q -> p j q", j=PACK))
+        load_scale_rows(nc, key_plane, keys_scales)
+        nc.sync.dma_start(
+            out=key_words[:].bitcast(I32),
+            in_=keys_words[0].rearrange("p t r -> p (t r)").bitcast(I32),
+        )
+        nc.sync.dma_start(out=note_words[:].bitcast(I32), in_=notes_words[0].bitcast(I32))
+        nc.sync.dma_start(token_list[:], offs)
+        load_scale_rows(nc, note_plane, notes_scales)
+        nc.sync.dma_start(minus_list[:], offs2)
+        nc.sync.dma_start(spread_list[:], offs3)
+        nc.sync.dma_start(result_list[:], offs4)
+        nc.gpsimd.memset(f1[:], 0.0)
+
+        q_grouped = sb.tile([P, Q, PACK], BF16, name="q_grouped", align_bytes=64)
+        nc.vector.tensor_copy(
+            out=q_grouped[:].rearrange("p (c i) j -> p c j i", i=4),
+            in_=q_raw[:].rearrange("p j (c i) -> p c j i", i=4),
+        )
+        q_codes = sb.tile([P, Q], U32, name="q_codes", align_bytes=64)
+        q_plane = sb.tile([P, Q], U8, name="q_plane", align_bytes=64)
+        nc.vector.quantize_mx(
+            out=q_codes[:].bitcast(FP8X4),
+            scales=q_plane[:],
+            in_=q_grouped[:].rearrange("p q j -> p (q j)"),
+        )
+
+        a = sb.tile([P, T], F32, name="a")
+        for piece in range(T // PIECE):
+            cols = slice(piece * PIECE, (piece + 1) * PIECE)
+            bank = psum.tile([P, PIECE], F32, name=f"a_bank{piece}")
+            nc.tensor.matmul_mx(
+                out=bank[:],
+                lhsT=q_codes[:].bitcast(FP8X4),
+                lhsT_scale=q_plane[:],
+                rhs=key_words[:, cols].bitcast(FP8X4),
+                rhs_scale=key_plane[:, cols],
+                start=True,
+                stop=True,
+            )
+            if piece % 2 == 0:
+                nc.vector.tensor_copy(out=a[:, cols], in_=bank[:])
+            else:
+                nc.scalar.copy(out=a[:, cols], in_=bank[:])
+
+        w = sb.tile([P, I], F32, name="w")
+        nc.vector.tensor_scalar(w[:], a[:].indirect(token_list[:]), W_SCALE, 0.0, MULT, ADD)
+        p2 = sb.tile([P, J], F32, name="p2")
+        nc.vector.tensor_tensor(p2[:], w[:, 0::2], w[:, 1::2], ADD)
+
+        b = sb.tile([P, U], F32, name="b")
+        for piece in range(U // PIECE):
+            cols = slice(piece * PIECE, (piece + 1) * PIECE)
+            bank = psum.tile([P, PIECE], F32, name=f"b_bank{piece}")
+            nc.tensor.matmul_mx(
+                out=bank[:],
+                lhsT=q_codes[:].bitcast(FP8X4),
+                lhsT_scale=q_plane[:],
+                rhs=note_words[:, 2 * piece * PIECE : 2 * (piece + 1) * PIECE].bitcast(FP4X4),
+                rhs_scale=note_plane[:, cols],
+                start=True,
+                stop=True,
+            )
+            nc.scalar.copy(out=b[:, cols], in_=bank[:])
+
+        minus_b = sb.tile([P, J], F32, name="minus_b")
+        nc.scalar.activation(minus_b[:], b[:].indirect(minus_list[:]), COPY, scale=-1.0)
+        nc.vector.tensor_tensor(f1[:].indirect(spread_list[:]), p2[:], minus_b[:], ADD)
+
+        bb = sb.tile([P, U], F32, name="bb")
+        nc.vector.tensor_tensor(bb[:], b[:], f1[:], ADD)
+
+        half = I // 2
+        first = sb.tile([P, half], F32, name="first")
+        nc.vector.tensor_tensor(first[:], bb[:].indirect(result_list[:, : half // 16]), w[:, :half], ADD)
+        nc.sync.dma_start(out=out[:, :half], in_=first[:])
+        picked = sb.tile([P, half], F32, name="picked")
+        nc.scalar.activation(picked[:], bb[:].indirect(result_list[:, half // 16 :]), COPY)
+        second = sb.tile([P, half], F32, name="second")
+        nc.vector.tensor_tensor(second[:], picked[:], w[:, half:], ADD)
+        nc.sync.dma_start(out=out[:, half:], in_=second[:])

@@ -46,7 +46,7 @@ def tile_attend_pairspread_two_kernel(
         result_list = lists.tile([P, I // 16], U16, name="result_list")
 
         q_raw = sb.tile([P, PACK, Q], F32, name="q_raw")
-        key_words = sb.tile([P, T], U32, name="key_words", align_bytes=64)
+        key_words = [sb.tile([P, T // 2], U32, name=f"key_words{h}", align_bytes=64) for h in range(2)]
         key_plane = sb.tile([P, T], U8, name="key_plane", align_bytes=64)
         note_words = sb.tile([P, 2 * U], U8, name="note_words", align_bytes=64)
         note_plane = sb.tile([P, U], U8, name="note_plane", align_bytes=64)
@@ -54,10 +54,9 @@ def tile_attend_pairspread_two_kernel(
 
         nc.sync.dma_start(out=q_raw[:], in_=query.rearrange("(p j) q -> p j q", j=PACK))
         load_scale_rows(nc, key_plane, keys_scales)
-        nc.sync.dma_start(
-            out=key_words[:].bitcast(I32),
-            in_=keys_words[0].rearrange("p t r -> p (t r)").bitcast(I32),
-        )
+        key_source = keys_words[0].rearrange("p t r -> p (t r)").bitcast(I32)
+        for h in range(2):
+            nc.sync.dma_start(out=key_words[h][:].bitcast(I32), in_=key_source[:, h * (T // 2) : (h + 1) * (T // 2)])
         nc.sync.dma_start(out=note_words[:].bitcast(I32), in_=notes_words[0].bitcast(I32))
         nc.sync.dma_start(token_list[:], offs)
         load_scale_rows(nc, note_plane, notes_scales)
@@ -87,7 +86,7 @@ def tile_attend_pairspread_two_kernel(
                 out=bank[:],
                 lhsT=q_codes[:].bitcast(FP8X4),
                 lhsT_scale=q_plane[:],
-                rhs=key_words[:, cols].bitcast(FP8X4),
+                rhs=key_words[piece // 2][:, (piece % 2) * PIECE : (piece % 2 + 1) * PIECE].bitcast(FP8X4),
                 rhs_scale=key_plane[:, cols],
                 start=True,
                 stop=True,
@@ -103,6 +102,7 @@ def tile_attend_pairspread_two_kernel(
         nc.vector.tensor_tensor(p2[:], w[:, 0::2], w[:, 1::2], ADD)
 
         b = sb.tile([P, U], F32, name="b")
+        b_banks = []
         for piece in range(U // PIECE):
             cols = slice(piece * PIECE, (piece + 1) * PIECE)
             bank = psum.tile([P, PIECE], F32, name=f"b_bank{piece}")
@@ -116,13 +116,18 @@ def tile_attend_pairspread_two_kernel(
                 stop=True,
             )
             nc.scalar.copy(out=b[:, cols], in_=bank[:])
+            b_banks.append(bank)
 
         minus_b = sb.tile([P, J], F32, name="minus_b")
         nc.scalar.activation(minus_b[:], b[:].indirect(minus_list[:]), COPY, scale=-1.0)
         nc.vector.tensor_tensor(f1[:].indirect(spread_list[:]), p2[:], minus_b[:], ADD)
 
         bb = sb.tile([P, U], F32, name="bb")
-        nc.vector.tensor_tensor(bb[:], b[:], f1[:], ADD)
+        last = slice(U - PIECE, U)
+        nc.gpsimd.tensor_tensor(bb[:, last], b[:, last], f1[:, last], ADD)
+        for piece in range(U // PIECE - 1):
+            cols = slice(piece * PIECE, (piece + 1) * PIECE)
+            nc.vector.tensor_tensor(bb[:, cols], b_banks[piece][:], f1[:, cols], ADD)
 
         half = I // 2
         first = sb.tile([P, half], F32, name="first")

@@ -23,9 +23,9 @@ PIECE = 256
 W_SCALE = 0.75
 
 
-def load_scale_rows(nc, plane, scales):
-    for quadrant in range(4):
-        nc.sync.dma_start(
+def load_scale_rows(queue, plane, scales, quadrants):
+    for quadrant in quadrants:
+        queue.dma_start(
             out=plane[32 * quadrant : 32 * quadrant + 4, :].bitcast(I32),
             in_=scales[0, 4 * quadrant : 4 * quadrant + 4, :].bitcast(I32),
         )
@@ -50,22 +50,21 @@ def tile_attend_pairspread_two_kernel(
         key_plane = sb.tile([P, T], U8, name="key_plane", align_bytes=64)
         note_words = sb.tile([P, 2 * U], U8, name="note_words", align_bytes=64)
         note_plane = sb.tile([P, U], U8, name="note_plane", align_bytes=64)
-        f1 = sb.tile([P, U], F32, name="f1")
 
         nc.sync.dma_start(out=q_raw[:], in_=query.rearrange("(p j) q -> p j q", j=PACK))
-        load_scale_rows(nc, key_plane, keys_scales)
+        load_scale_rows(nc.sync, key_plane, keys_scales, range(4))
+        load_scale_rows(nc.gpsimd, note_plane, notes_scales, range(2))
         key_source = keys_words[0].rearrange("p t r -> p (t r)").bitcast(I32)
         for h in range(2):
             nc.sync.dma_start(out=key_words[h][:].bitcast(I32), in_=key_source[:, h * (T // 2) : (h + 1) * (T // 2)])
         nc.sync.dma_start(out=note_words[:].bitcast(I32), in_=notes_words[0].bitcast(I32))
+        load_scale_rows(nc.sync, note_plane, notes_scales, range(2, 4))
         nc.sync.dma_start(token_list[:], offs)
-        load_scale_rows(nc, note_plane, notes_scales)
         nc.sync.dma_start(minus_list[:], offs2)
         nc.sync.dma_start(spread_list[:], offs3)
         nc.sync.dma_start(result_list[:], offs4)
-        nc.gpsimd.memset(f1[:], 0.0)
 
-        q_grouped = sb.tile([P, Q, PACK], BF16, name="q_grouped", align_bytes=64)
+        q_grouped = sb.tile([P, Q, PACK], BF16, name="q_grouped", tag="grouped_then_f1", align_bytes=64)
         nc.vector.tensor_copy(
             out=q_grouped[:].rearrange("p (c i) j -> p c j i", i=4),
             in_=q_raw[:].rearrange("p j (c i) -> p c j i", i=4),
@@ -77,6 +76,9 @@ def tile_attend_pairspread_two_kernel(
             scales=q_plane[:],
             in_=q_grouped[:].rearrange("p q j -> p (q j)"),
         )
+
+        f1 = sb.tile([P, U], F32, name="f1", tag="grouped_then_f1", align_bytes=64)
+        nc.gpsimd.memset(f1[:], 0.0)
 
         a = sb.tile([P, T], F32, name="a")
         for piece in range(T // PIECE):

from contextlib import ExitStack

import concourse.mybir as mybir

D, T, U, I, J, Q = 512, 1024, 1024, 512, 256, 128
FLOPS = 2 * D * Q * (T + U)

F32 = mybir.dt.float32
BF16 = mybir.dt.bfloat16
I32 = mybir.dt.int32
U32 = mybir.dt.uint32
U16 = mybir.dt.uint16
U8 = mybir.dt.uint8
FP8X4 = mybir.dt.float8_e4m3fn_x4
FP4X4 = mybir.dt.float4_e2m1fn_x4
ADD = mybir.AluOpType.add
MULT = mybir.AluOpType.mult
COPY = mybir.ActivationFunctionType.Copy

P = 128
PACK = 4
PIECE = 256
W_SCALE = 0.75


def load_scale_rows(queue, plane, scales, quadrants):
    for quadrant in quadrants:
        queue.dma_start(
            out=plane[32 * quadrant : 32 * quadrant + 4, :].bitcast(I32),
            in_=scales[0, 4 * quadrant : 4 * quadrant + 4, :].bitcast(I32),
        )


def tile_attend_pairspread_two_kernel(
    tc, query, keys_words, keys_scales, notes_words, notes_scales, offs, offs2, offs3, offs4, out
):
    nc = tc.nc
    with ExitStack() as ctx:
        lists = ctx.enter_context(tc.tile_pool(name="lists", bufs=1))
        sb = ctx.enter_context(tc.tile_pool(name="sb", bufs=1))
        psum = ctx.enter_context(tc.psum_pool(name="psum", bufs=1))

        token_list = lists.tile([P, I // 16], U16, name="token_list")
        minus_list = lists.tile([P, J // 16], U16, name="minus_list")
        spread_list = lists.tile([P, J // 16], U16, name="spread_list")
        result_list = lists.tile([P, I // 16], U16, name="result_list")

        q_raw = sb.tile([P, PACK, Q], F32, name="q_raw")
        key_words = [sb.tile([P, T // 2], U32, name=f"key_words{h}", align_bytes=64) for h in range(2)]
        key_plane = sb.tile([P, T], U8, name="key_plane", align_bytes=64)
        note_words = sb.tile([P, 2 * U], U8, name="note_words", align_bytes=64)
        note_plane = sb.tile([P, U], U8, name="note_plane", align_bytes=64)

        nc.sync.dma_start(out=q_raw[:], in_=query.rearrange("(p j) q -> p j q", j=PACK))
        load_scale_rows(nc.sync, key_plane, keys_scales, range(4))
        load_scale_rows(nc.gpsimd, note_plane, notes_scales, range(2))
        key_source = keys_words[0].rearrange("p t r -> p (t r)").bitcast(I32)
        for h in range(2):
            nc.sync.dma_start(out=key_words[h][:].bitcast(I32), in_=key_source[:, h * (T // 2) : (h + 1) * (T // 2)])
        nc.sync.dma_start(out=note_words[:].bitcast(I32), in_=notes_words[0].bitcast(I32))
        load_scale_rows(nc.sync, note_plane, notes_scales, range(2, 4))
        nc.sync.dma_start(token_list[:], offs)
        nc.sync.dma_start(minus_list[:], offs2)
        nc.sync.dma_start(spread_list[:], offs3)
        nc.sync.dma_start(result_list[:], offs4)

        q_grouped = sb.tile([P, Q, PACK], BF16, name="q_grouped", tag="grouped_then_f1", align_bytes=64)
        nc.vector.tensor_copy(
            out=q_grouped[:].rearrange("p (c i) j -> p c j i", i=4),
            in_=q_raw[:].rearrange("p j (c i) -> p c j i", i=4),
        )
        q_codes = sb.tile([P, Q], U32, name="q_codes", align_bytes=64)
        q_plane = sb.tile([P, Q], U8, name="q_plane", align_bytes=64)
        nc.vector.quantize_mx(
            out=q_codes[:].bitcast(FP8X4),
            scales=q_plane[:],
            in_=q_grouped[:].rearrange("p q j -> p (q j)"),
        )

        f1 = sb.tile([P, U], F32, name="f1", tag="grouped_then_f1", align_bytes=64)
        nc.gpsimd.memset(f1[:], 0.0)

        a = sb.tile([P, T], F32, name="a")
        for piece in range(T // PIECE):
            cols = slice(piece * PIECE, (piece + 1) * PIECE)
            bank = psum.tile([P, PIECE], F32, name=f"a_bank{piece}")
            nc.tensor.matmul_mx(
                out=bank[:],
                lhsT=q_codes[:].bitcast(FP8X4),
                lhsT_scale=q_plane[:],
                rhs=key_words[piece // 2][:, (piece % 2) * PIECE : (piece % 2 + 1) * PIECE].bitcast(FP8X4),
                rhs_scale=key_plane[:, cols],
                start=True,
                stop=True,
            )
            if piece % 2 == 0:
                nc.vector.tensor_copy(out=a[:, cols], in_=bank[:])
            else:
                nc.scalar.copy(out=a[:, cols], in_=bank[:])

        w = sb.tile([P, I], F32, name="w")
        nc.vector.tensor_scalar(w[:], a[:].indirect(token_list[:]), W_SCALE, 0.0, MULT, ADD)
        p2 = sb.tile([P, J], F32, name="p2")
        nc.vector.tensor_tensor(p2[:], w[:, 0::2], w[:, 1::2], ADD)

        b = sb.tile([P, U], F32, name="b")
        b_banks = []
        for piece in range(U // PIECE):
            cols = slice(piece * PIECE, (piece + 1) * PIECE)
            bank = psum.tile([P, PIECE], F32, name=f"b_bank{piece}")
            nc.tensor.matmul_mx(
                out=bank[:],
                lhsT=q_codes[:].bitcast(FP8X4),
                lhsT_scale=q_plane[:],
                rhs=note_words[:, 2 * piece * PIECE : 2 * (piece + 1) * PIECE].bitcast(FP4X4),
                rhs_scale=note_plane[:, cols],
                start=True,
                stop=True,
            )
            nc.scalar.copy(out=b[:, cols], in_=bank[:])
            b_banks.append(bank)

        minus_b = sb.tile([P, J], F32, name="minus_b")
        nc.scalar.activation(minus_b[:], b[:].indirect(minus_list[:]), COPY, scale=-1.0)
        nc.vector.tensor_tensor(f1[:].indirect(spread_list[:]), p2[:], minus_b[:], ADD)

        bb = sb.tile([P, U], F32, name="bb")
        last = slice(U - PIECE, U)
        nc.gpsimd.tensor_tensor(bb[:, last], b[:, last], f1[:, last], ADD)
        for piece in range(U // PIECE - 1):
            cols = slice(piece * PIECE, (piece + 1) * PIECE)
            nc.vector.tensor_tensor(bb[:, cols], b_banks[piece][:], f1[:, cols], ADD)

        half = I // 2
        first = sb.tile([P, half], F32, name="first")
        nc.vector.tensor_tensor(first[:], bb[:].indirect(result_list[:, : half // 16]), w[:, :half], ADD)
        nc.sync.dma_start(out=out[:, :half], in_=first[:])
        picked = sb.tile([P, half], F32, name="picked")
        nc.scalar.activation(picked[:], bb[:].indirect(result_list[:, half // 16 :]), COPY)
        second = sb.tile([P, half], F32, name="second")
        nc.vector.tensor_tensor(second[:], picked[:], w[:, half:], ADD)
        nc.sync.dma_start(out=out[:, half:], in_=second[:])
